import numpy as np
import ml_dtypes


def mxq(x, axis, fmt="e4m3"):
    dtype, down = {"e4m3": (ml_dtypes.float8_e4m3fn, 7), "e5m2": (ml_dtypes.float8_e5m2, 14)}[fmt]
    v = np.moveaxis(np.asarray(x, np.float32).astype(ml_dtypes.bfloat16).astype(np.float64), axis, -1)
    blocks = v.reshape(v.shape[:-1] + (-1, 32))
    amax = np.abs(blocks).max(-1, keepdims=True)
    byte = np.maximum(np.where(amax > 0, np.frexp(amax)[1] - 1 + 127, 0) - down, 1)
    scale = np.exp2(byte - 127.0)
    codes = (blocks / scale).astype(np.float32).astype(dtype).astype(np.float64)
    return np.moveaxis((codes * scale).reshape(v.shape), -1, axis)


WIDE = False


def mx_kscale(k):
    if not WIDE:
        return np.ones(k)
    levels = np.array([30, -30])
    if k % 512:
        return np.exp2(np.random.permutation(np.resize(levels, k // 32))).repeat(32)
    a = np.empty((k // 512, 16))
    for p in range(k // 512):
        a[p, :8] = np.random.permutation(np.resize(levels, 8))
        for g in range(8):
            far = levels[np.abs(levels - a[p, g]) >= 10]
            a[p, g + 8] = far[np.random.randint(len(far))]
    return np.exp2(a.ravel()).repeat(32)


BF16 = ml_dtypes.bfloat16


def bf(x):
    return np.asarray(x, np.float32).astype(BF16)


def f64(x):
    return np.asarray(x).astype(np.float64)


E2M1 = np.array([0.0, 0.5, 1.0, 1.5, 2.0, 3.0, 4.0, 6.0, -0.0, -0.5, -1.0, -1.5, -2.0, -3.0, -4.0, -6.0])


def pack_weight(w, fmt):
    k, n = w.shape
    w = f64(bf(w)).reshape(k // 32, 32, n)
    amax = np.abs(w).max(1)
    if fmt in ("e4m3", "e5m2"):
        byte = np.frexp(amax)[1] - 1 + 127 - (7 if fmt == "e4m3" else 14)
    else:
        mant, ex = np.frexp(amax / 6.0)
        byte = np.where(mant > 0.5, ex, ex - 1) + 127
    byte = np.clip(np.where(amax > 0, byte, 1), 1, 254)
    scaled = (w * np.exp2(127.0 - byte)[:, None, :]).reshape(k, n).astype(np.float32)
    by_word = np.ascontiguousarray(scaled.reshape(k // 512, 128, 4, n).transpose(0, 1, 3, 2))
    if fmt in ("e4m3", "e5m2"):
        words = by_word.astype(ml_dtypes.float8_e4m3fn if fmt == "e4m3" else ml_dtypes.float8_e5m2).view(np.uint8)
    else:
        c = by_word.astype(ml_dtypes.float4_e2m1fn).view(np.uint8) & 0xF
        words = c[..., 0::2] | (c[..., 1::2] << 4)
    return np.ascontiguousarray(words), np.ascontiguousarray(byte.astype(np.uint8).reshape(k // 512, 16, n))


def unpack_weight(words, scales, fmt):
    g, p, n, _ = words.shape
    if fmt in ("e4m3", "e5m2"):
        vals = np.ascontiguousarray(words).view(ml_dtypes.float8_e4m3fn if fmt == "e4m3" else ml_dtypes.float8_e5m2).astype(np.float64)
    else:
        nib = np.empty((g, p, n, 4), np.uint8)
        nib[..., 0::2] = words & 0xF
        nib[..., 1::2] = words >> 4
        vals = E2M1[nib]
    vals = vals * np.repeat(np.exp2(scales.astype(np.float64) - 127.0), 8, axis=1)[..., None]
    return vals.transpose(0, 1, 3, 2).reshape(g * 512, n)


M, V, D = 1024, 2048, 1024


def setup_inputs():
    s = mx_kscale(M)
    t = mx_kscale(V)
    err = np.random.standard_normal((M, V)) * np.exp(0.5 * np.random.standard_normal((M, V))) / np.sqrt(M)
    G_words, G_scales = pack_weight(err * s[:, None], "e5m2")
    T_words, T_scales = pack_weight(err.T * t[:, None], "e5m2")
    return {"g_words": G_words, "g_scales": G_scales,
            "t_words": T_words, "t_scales": T_scales,
            "h": bf(np.random.standard_normal((M, D)) / s[:, None]),
            "u": bf(np.random.standard_normal((D, V)) * np.sqrt(M / V) / t),
            "acc": bf(0.5 * np.random.standard_normal((D, V))),
            "gain": bf(1 + 0.1 * np.random.standard_normal(D))}


def reference(g_words, g_scales, t_words, t_scales, h, u, acc, gain):
    G = unpack_weight(g_words, g_scales, "e5m2")
    T = unpack_weight(t_words, t_scales, "e5m2")
    du = (mxq(f64(h), 0, "e4m3").T @ G) + f64(acc)
    dh = T.T @ mxq(f64(u), 1, "e4m3").T
    dx = dh * f64(gain)[None, :]
    return du, dx

@@ -1,0 +1,232 @@
+from contextlib import ExitStack
+
+import concourse.mybir as mybir
+from concourse.masks import make_identity
+
+TOKENS, VOCAB, FEATURES = 1024, 2048, 1024
+FLOPS = 2 * 2 * TOKENS * VOCAB * FEATURES
+
+F32 = mybir.dt.float32
+BF16 = mybir.dt.bfloat16
+U32 = mybir.dt.uint32
+I32 = mybir.dt.int32
+U8 = mybir.dt.uint8
+E4M3 = mybir.dt.float8_e4m3fn_x4
+E5M2 = mybir.dt.float8_e5m2_x4
+ADD = mybir.AluOpType.add
+MULT = mybir.AluOpType.mult
+
+P = 128
+PACK = 4
+K_PASS = P * PACK
+N = 512
+PAIR = 2 * P
+PAIRS = FEATURES // PAIR
+TOK_PASSES = TOKENS // K_PASS
+VOC_PASSES = VOCAB // K_PASS
+TOK_TILES = TOKENS // P
+
+
+def tile_unembedding_backward_planes_e1_kernel(
+    tc, g_words, g_scales, t_words, t_scales, h, u, acc, gain, du, dx
+):
+    nc = tc.nc
+    with ExitStack() as ctx:
+        ctx.enter_context(tc.manual_schedule())
+        keep = ctx.enter_context(tc.tile_pool(name="keep", bufs=1))
+        stage = ctx.enter_context(tc.tile_pool(name="stage", bufs=4))
+        work = ctx.enter_context(tc.tile_pool(name="work", bufs=4))
+        dx_pool = ctx.enter_context(tc.tile_pool(name="dx_pool", bufs=6))
+        du_pool = ctx.enter_context(tc.tile_pool(name="du_pool", bufs=4))
+        psum = ctx.enter_context(tc.psum_pool(name="psum", bufs=8))
+
+        t_codes = keep.tile([P, VOC_PASSES, TOKENS], U32, name="t_codes", align_bytes=64)
+        t_plane = keep.tile([P, VOC_PASSES, TOKENS], U8, name="t_plane", align_bytes=64)
+        g_codes = keep.tile([P, TOK_PASSES, VOCAB], U32, name="g_codes", align_bytes=64)
+        g_plane = keep.tile([P, TOK_PASSES, VOCAB], U8, name="g_plane", align_bytes=64)
+        u_codes = keep.tile([P, VOC_PASSES, FEATURES], U32, name="u_codes", align_bytes=64)
+        u_plane = keep.tile([P, VOC_PASSES, FEATURES], U8, name="u_plane", align_bytes=64)
+        h_codes = keep.tile([P, TOK_PASSES, FEATURES], U32, name="h_codes", align_bytes=64)
+        h_plane = keep.tile([P, TOK_PASSES, FEATURES], U8, name="h_plane", align_bytes=64)
+        h_raw = keep.tile([P, TOK_PASSES, PACK, FEATURES], BF16, name="h_raw", align_bytes=64)
+        ident = keep.tile([P, P], F32, name="ident")
+        gain_bf = keep.tile([P, P], BF16, name="gain_bf")
+        gain_rows = keep.tile([P, P], F32, name="gain_rows")
+        gain_cols = keep.tile([P, FEATURES // P], F32, name="gain_cols")
+        gain_all = keep.tile([P, FEATURES], F32, name="gain_all")
+
+        u_raw = []
+        for b in range(PAIRS):
+            raw = stage.tile([P, 2, VOCAB], BF16, name="raw", align_bytes=64)
+            nc.sync.dma_start(
+                out=raw[:], in_=u[b * PAIR : (b + 1) * PAIR, :].rearrange("(p e) v -> p e v", e=2)
+            )
+            u_raw.append(raw)
+        for g in range(VOC_PASSES):
+            nc.sync.dma_start(
+                out=t_codes[:, g, :].bitcast(I32),
+                in_=t_words[g].rearrange("p n t -> p (n t)").bitcast(I32),
+            )
+        for g in range(TOK_PASSES):
+            nc.sync.dma_start(
+                out=h_raw[:, g, :, :],
+                in_=h[g * K_PASS : (g + 1) * K_PASS, :].rearrange("(p j) d -> p j d", j=PACK),
+            )
+        for g in range(TOK_PASSES):
+            nc.sync.dma_start(
+                out=g_codes[:, g, :].bitcast(I32),
+                in_=g_words[g].rearrange("p n t -> p (n t)").bitcast(I32),
+            )
+
+        nc.vector.memset(t_plane[:].rearrange("p g n -> p (g n)").bitcast(I32), 0)
+        nc.vector.memset(gain_bf[:], 0.0)
+        nc.vector.memset(g_plane[:].rearrange("p g n -> p (g n)").bitcast(I32), 0)
+        nc.scalar.dma_start(out=gain_bf[0 : FEATURES // P, :], in_=gain.rearrange("(c p) -> c p", p=P))
+        make_identity(nc, ident[:])
+        for plane, rows in ((t_plane, t_scales), (g_plane, g_scales)):
+            for r in range(PACK):
+                nc.gpsimd.dma_start(
+                    out=plane[r:P:32, :, :].bitcast(I32),
+                    in_=rows.bitcast(I32).rearrange("g (q r) n -> r q g n", r=PACK)[r],
+                )
+
+        def quantise_u(b):
+            words = u_raw[b][:].rearrange("p e v -> p (e v)").bitcast(F32).rearrange("p (e w) -> p e w", e=2)
+            grouped = []
+            for g in range(VOC_PASSES):
+                bank = psum.tile([P, 4, P], F32, name="bank", tag="bank")
+                for e in range(2):
+                    for half in range(2):
+                        nc.tensor.transpose(
+                            bank[:, 2 * e + half, :],
+                            words[:, e, g * PAIR + half : (g + 1) * PAIR : 2],
+                            ident[:],
+                        )
+                tile = work.tile([P, PAIR * PACK], BF16, name="u_grouped", align_bytes=64)
+                src = bank[:].rearrange("p q r -> p r q")
+                dst = tile[:].bitcast(F32).rearrange("p (r q) -> p r q", q=4)
+                if g % 2 == 0:
+                    nc.scalar.copy(out=dst, in_=src)
+                else:
+                    nc.vector.tensor_copy(out=dst, in_=src)
+                grouped.append(tile)
+            for g in range(VOC_PASSES):
+                cols = slice(b * PAIR, (b + 1) * PAIR)
+                nc.vector.quantize_mx(
+                    out=u_codes[:, g, cols].bitcast(E4M3), scales=u_plane[:, g, cols], in_=grouped[g][:]
+                )
+
+        for b in range(PAIRS):
+            quantise_u(b)
+
+        nc.vector.tensor_copy(out=gain_rows[:], in_=gain_bf[:])
+        bank = psum.tile([P, 4, P], F32, name="bank", tag="bank")
+        nc.tensor.transpose(bank[:, 0, :], gain_rows[:], ident[:])
+        nc.vector.tensor_copy(out=gain_cols[:], in_=bank[:, 0, 0 : FEATURES // P])
+        for c0 in range(0, FEATURES // P, 4):
+            bank = psum.tile([P, 4, P], F32, name="bank", tag="bank")
+            for c in range(4):
+                nc.tensor.transpose(
+                    bank[:, c, :], gain_cols[:, c0 + c : c0 + c + 1].to_broadcast([P, P]), ident[:]
+                )
+            nc.scalar.copy(
+                out=gain_all[:, c0 * P : (c0 + 4) * P], in_=bank[:].rearrange("p q r -> p (q r)")
+            )
+
+        def quantise_h(g, half):
+            tile = work.tile([P, N, PACK], BF16, name="h_grouped", bufs=2, align_bytes=64)
+            for b in range(2):
+                src = h_raw[:, g, :, (2 * half + b) * PAIR : (2 * half + b + 1) * PAIR]
+                nc.scalar.copy(
+                    out=tile[:, b * PAIR : (b + 1) * PAIR, :].rearrange("p (e m) j -> p e m j", e=2),
+                    in_=src.rearrange("p j (m e) -> p e m j", e=2),
+                )
+            cols = slice(half * N, (half + 1) * N)
+            nc.vector.quantize_mx(
+                out=h_codes[:, g, cols].bitcast(E4M3),
+                scales=h_plane[:, g, cols],
+                in_=tile[:].rearrange("p c j -> p (c j)"),
+            )
+
+        acc_raw = []
+
+        def load_acc(b):
+            raw = stage.tile([P, 2, VOCAB], BF16, name="raw", align_bytes=64)
+            nc.sync.dma_start(
+                out=raw[:], in_=acc[b * PAIR : (b + 1) * PAIR, :].rearrange("(p e) v -> p e v", e=2)
+            )
+            acc_raw.append(raw)
+
+        def dx_rows(m):
+            toks = slice(m * P, (m + 1) * P)
+            dx_tile = dx_pool.tile([P, FEATURES], F32, name="dx_tile", align_bytes=64)
+            for f in range(2):
+                cols = slice(f * N, (f + 1) * N)
+                prod = psum.tile([P, N], F32, name="prod", tag="bank")
+                for g in range(VOC_PASSES):
+                    nc.tensor.matmul_mx(
+                        out=prod[:],
+                        lhsT=t_codes[:, g, toks].bitcast(E5M2),
+                        lhsT_scale=t_plane[:, g, toks],
+                        rhs=u_codes[:, g, cols].bitcast(E4M3),
+                        rhs_scale=u_plane[:, g, cols],
+                        start=(g == 0),
+                        stop=(g == VOC_PASSES - 1),
+                    )
+                nc.vector.tensor_tensor(out=dx_tile[:, cols], in0=prod[:], in1=gain_all[:, cols], op=MULT)
+            nc.sync.dma_start(out=dx[toks, :], in_=dx_tile[:])
+
+        du_tiles = []
+
+        def du_rows(b, e):
+            if e == 0:
+                new_tile = du_pool.tile([P, 2, VOCAB], F32, name="du_tile", align_bytes=64)
+                du_tiles.append(new_tile)
+            du_tile = du_tiles[b]
+            feats = slice((2 * b + e) * P, (2 * b + e + 1) * P)
+            for n in range(VOCAB // N):
+                cols = slice(n * N, (n + 1) * N)
+                prod = psum.tile([P, N], F32, name="prod", tag="bank")
+                for g in range(TOK_PASSES):
+                    nc.tensor.matmul_mx(
+                        out=prod[:],
+                        lhsT=h_codes[:, g, feats].bitcast(E4M3),
+                        lhsT_scale=h_plane[:, g, feats],
+                        rhs=g_codes[:, g, cols].bitcast(E5M2),
+                        rhs_scale=g_plane[:, g, cols],
+                        start=(g == 0),
+                        stop=(g == TOK_PASSES - 1),
+                    )
+                nc.vector.tensor_tensor(
+                    out=du_tile[:, e, cols], in0=prod[:], in1=acc_raw[b][:, e, cols], op=ADD
+                )
+            rows = du[b * PAIR : (b + 1) * PAIR, :].rearrange("(p e) v -> p e v", e=2)
+            if b == PAIRS - 1:
+                nc.sync.dma_start(out=rows[:, e, :], in_=du_tile[:, e, :])
+            elif e == 1:
+                nc.sync.dma_start(out=rows, in_=du_tile[:])
+
+        load_acc(0)
+        dx_rows(0)
+        dx_rows(1)
+        load_acc(1)
+        dx_rows(2)
+        quantise_h(0, 0)
+        dx_rows(3)
+        quantise_h(1, 0)
+        load_acc(2)
+        dx_rows(4)
+        quantise_h(0, 1)
+        load_acc(3)
+        du_rows(0, 0)
+        quantise_h(1, 1)
+        dx_rows(5)
+        du_rows(0, 1)
+        dx_rows(6)
+        du_rows(1, 0)
+        dx_rows(7)
+        du_rows(1, 1)
+        du_rows(2, 0)
+        du_rows(2, 1)
+        du_rows(3, 0)
+        du_rows(3, 1)

@@ -36,11 +36,14 @@ def tile_unembedding_backward_planes_e1_kernel(
         keep = ctx.enter_context(tc.tile_pool(name="keep", bufs=1))
         stage = ctx.enter_context(tc.tile_pool(name="stage", bufs=4))
         work = ctx.enter_context(tc.tile_pool(name="work", bufs=4))
-        dx_pool = ctx.enter_context(tc.tile_pool(name="dx_pool", bufs=6))
-        du_pool = ctx.enter_context(tc.tile_pool(name="du_pool", bufs=4))
+        dx_pool = ctx.enter_context(tc.tile_pool(name="dx_pool", bufs=7))
+        du_pool = ctx.enter_context(tc.tile_pool(name="du_pool", bufs=6))
         psum = ctx.enter_context(tc.psum_pool(name="psum", bufs=8))
 
-        t_codes = keep.tile([P, VOC_PASSES, TOKENS], U32, name="t_codes", align_bytes=64)
+        t_codes = []
+        for part in range(TOKENS // N):
+            codes = keep.tile([P, VOC_PASSES, N], U32, name="t_codes_%d" % part, align_bytes=64)
+            t_codes.append(codes)
         t_plane = keep.tile([P, VOC_PASSES, TOKENS], U8, name="t_plane", align_bytes=64)
         g_codes = keep.tile([P, TOK_PASSES, VOCAB], U32, name="g_codes", align_bytes=64)
         g_plane = keep.tile([P, TOK_PASSES, VOCAB], U8, name="g_plane", align_bytes=64)
@@ -56,17 +59,27 @@ def tile_unembedding_backward_planes_e1_kernel(
         gain_all = keep.tile([P, FEATURES], F32, name="gain_all")
 
         u_raw = []
-        for b in range(PAIRS):
+
+        def load_u(b):
             raw = stage.tile([P, 2, VOCAB], BF16, name="raw", align_bytes=64)
             nc.sync.dma_start(
                 out=raw[:], in_=u[b * PAIR : (b + 1) * PAIR, :].rearrange("(p e) v -> p e v", e=2)
             )
             u_raw.append(raw)
-        for g in range(VOC_PASSES):
+
+        def load_t(part):
+            toks = slice(part * N, (part + 1) * N)
             nc.sync.dma_start(
-                out=t_codes[:, g, :].bitcast(I32),
-                in_=t_words[g].rearrange("p n t -> p (n t)").bitcast(I32),
+                out=t_codes[part][:].bitcast(I32),
+                in_=t_words.rearrange("g p n t -> p g (n t)").bitcast(I32)[:, :, toks],
             )
+
+        load_u(0)
+        load_u(1)
+        load_t(0)
+        load_u(2)
+        load_u(3)
+        load_t(1)
         for g in range(TOK_PASSES):
             nc.sync.dma_start(
                 out=h_raw[:, g, :, :],
@@ -83,9 +96,9 @@ def tile_unembedding_backward_planes_e1_kernel(
         nc.vector.memset(g_plane[:].rearrange("p g n -> p (g n)").bitcast(I32), 0)
         nc.scalar.dma_start(out=gain_bf[0 : FEATURES // P, :], in_=gain.rearrange("(c p) -> c p", p=P))
         make_identity(nc, ident[:])
-        for plane, rows in ((t_plane, t_scales), (g_plane, g_scales)):
+        for queue, plane, rows in ((nc.scalar, t_plane, t_scales), (nc.gpsimd, g_plane, g_scales)):
             for r in range(PACK):
-                nc.gpsimd.dma_start(
+                queue.dma_start(
                     out=plane[r:P:32, :, :].bitcast(I32),
                     in_=rows.bitcast(I32).rearrange("g (q r) n -> r q g n", r=PACK)[r],
                 )
@@ -116,8 +129,7 @@ def tile_unembedding_backward_planes_e1_kernel(
                     out=u_codes[:, g, cols].bitcast(E4M3), scales=u_plane[:, g, cols], in_=grouped[g][:]
                 )
 
-        for b in range(PAIRS):
-            quantise_u(b)
+        quantise_u(0)
 
         nc.vector.tensor_copy(out=gain_rows[:], in_=gain_bf[:])
         bank = psum.tile([P, 4, P], F32, name="bank", tag="bank")
@@ -132,6 +144,8 @@ def tile_unembedding_backward_planes_e1_kernel(
             nc.scalar.copy(
                 out=gain_all[:, c0 * P : (c0 + 4) * P], in_=bank[:].rearrange("p q r -> p (q r)")
             )
+
+        quantise_u(1)
 
         def quantise_h(g, half):
             tile = work.tile([P, N, PACK], BF16, name="h_grouped", bufs=2, align_bytes=64)
@@ -157,32 +171,36 @@ def tile_unembedding_backward_planes_e1_kernel(
             )
             acc_raw.append(raw)
 
-        def dx_rows(m):
-            toks = slice(m * P, (m + 1) * P)
-            dx_tile = dx_pool.tile([P, FEATURES], F32, name="dx_tile", align_bytes=64)
-            for f in range(2):
-                cols = slice(f * N, (f + 1) * N)
-                prod = psum.tile([P, N], F32, name="prod", tag="bank")
-                for g in range(VOC_PASSES):
-                    nc.tensor.matmul_mx(
-                        out=prod[:],
-                        lhsT=t_codes[:, g, toks].bitcast(E5M2),
-                        lhsT_scale=t_plane[:, g, toks],
-                        rhs=u_codes[:, g, cols].bitcast(E4M3),
-                        rhs_scale=u_plane[:, g, cols],
-                        start=(g == 0),
-                        stop=(g == VOC_PASSES - 1),
-                    )
-                nc.vector.tensor_tensor(out=dx_tile[:, cols], in0=prod[:], in1=gain_all[:, cols], op=MULT)
-            nc.sync.dma_start(out=dx[toks, :], in_=dx_tile[:])
+        dx_tiles = {}
 
-        du_tiles = []
+        def dx_part(m, f):
+            toks = slice(m * P, (m + 1) * P)
+            if f == 0:
+                new_tile = dx_pool.tile([P, FEATURES], F32, name="dx_tile", align_bytes=64)
+                dx_tiles[m] = new_tile
+            dx_tile = dx_tiles[m]
+            cols = slice(f * N, (f + 1) * N)
+            prod = psum.tile([P, N], F32, name="prod", tag="bank")
+            for g in range(VOC_PASSES):
+                nc.tensor.matmul_mx(
+                    out=prod[:],
+                    lhsT=t_codes[m // 4][:, g, (m % 4) * P : (m % 4 + 1) * P].bitcast(E5M2),
+                    lhsT_scale=t_plane[:, g, toks],
+                    rhs=u_codes[:, g, cols].bitcast(E4M3),
+                    rhs_scale=u_plane[:, g, cols],
+                    start=(g == 0),
+                    stop=(g == VOC_PASSES - 1),
+                )
+            nc.vector.tensor_tensor(out=dx_tile[:, cols], in0=prod[:], in1=gain_all[:, cols], op=MULT)
+            if f == 1:
+                nc.sync.dma_start(out=dx[toks, :], in_=dx_tile[:])
+
+        def dx_rows(m):
+            dx_part(m, 0)
+            dx_part(m, 1)
 
         def du_rows(b, e):
-            if e == 0:
-                new_tile = du_pool.tile([P, 2, VOCAB], F32, name="du_tile", align_bytes=64)
-                du_tiles.append(new_tile)
-            du_tile = du_tiles[b]
+            du_tile = du_pool.tile([P, VOCAB], F32, name="du_tile", align_bytes=64)
             feats = slice((2 * b + e) * P, (2 * b + e + 1) * P)
             for n in range(VOCAB // N):
                 cols = slice(n * N, (n + 1) * N)
@@ -198,35 +216,35 @@ def tile_unembedding_backward_planes_e1_kernel(
                         stop=(g == TOK_PASSES - 1),
                     )
                 nc.vector.tensor_tensor(
-                    out=du_tile[:, e, cols], in0=prod[:], in1=acc_raw[b][:, e, cols], op=ADD
+                    out=du_tile[:, cols], in0=prod[:], in1=acc_raw[b][:, e, cols], op=ADD
                 )
             rows = du[b * PAIR : (b + 1) * PAIR, :].rearrange("(p e) v -> p e v", e=2)
-            if b == PAIRS - 1:
-                nc.sync.dma_start(out=rows[:, e, :], in_=du_tile[:, e, :])
-            elif e == 1:
-                nc.sync.dma_start(out=rows, in_=du_tile[:])
+            nc.sync.dma_start(out=rows[:, e, :], in_=du_tile[:])
 
+        dx_part(0, 0)
+        dx_part(1, 0)
+        quantise_u(2)
+        dx_part(2, 0)
+        dx_part(3, 0)
+        quantise_u(3)
         load_acc(0)
-        dx_rows(0)
-        dx_rows(1)
         load_acc(1)
-        dx_rows(2)
-        quantise_h(0, 0)
-        dx_rows(3)
-        quantise_h(1, 0)
+        dx_part(0, 1)
+        dx_part(1, 1)
+        dx_part(2, 1)
         load_acc(2)
+        dx_part(3, 1)
         dx_rows(4)
-        quantise_h(0, 1)
+        quantise_h(0, 0)
         load_acc(3)
+        dx_rows(5)
+        quantise_h(1, 0)
+        dx_rows(6)
+        quantise_h(0, 1)
         du_rows(0, 0)
         quantise_h(1, 1)
-        dx_rows(5)
-        du_rows(0, 1)
-        dx_rows(6)
-        du_rows(1, 0)
         dx_rows(7)
-        du_rows(1, 1)
-        du_rows(2, 0)
-        du_rows(2, 1)
-        du_rows(3, 0)
-        du_rows(3, 1)
+        for b in range(PAIRS):
+            for e in range(2):
+                if (b, e) != (0, 0):
+                    du_rows(b, e)

@@ -34,10 +34,10 @@ def tile_unembedding_backward_planes_e1_kernel(
     with ExitStack() as ctx:
         ctx.enter_context(tc.manual_schedule())
         keep = ctx.enter_context(tc.tile_pool(name="keep", bufs=1))
-        stage = ctx.enter_context(tc.tile_pool(name="stage", bufs=4))
+        stage = ctx.enter_context(tc.tile_pool(name="stage", bufs=2))
         work = ctx.enter_context(tc.tile_pool(name="work", bufs=4))
-        dx_pool = ctx.enter_context(tc.tile_pool(name="dx_pool", bufs=7))
-        du_pool = ctx.enter_context(tc.tile_pool(name="du_pool", bufs=6))
+        dx_pool = ctx.enter_context(tc.tile_pool(name="dx_pool", bufs=4))
+        du_pool = ctx.enter_context(tc.tile_pool(name="du_pool", bufs=3))
         psum = ctx.enter_context(tc.psum_pool(name="psum", bufs=8))
 
         t_codes = []
@@ -60,12 +60,13 @@ def tile_unembedding_backward_planes_e1_kernel(
 
         u_raw = []
 
-        def load_u(b):
-            raw = stage.tile([P, 2, VOCAB], BF16, name="raw", align_bytes=64)
-            nc.sync.dma_start(
-                out=raw[:], in_=u[b * PAIR : (b + 1) * PAIR, :].rearrange("(p e) v -> p e v", e=2)
-            )
-            u_raw.append(raw)
+        def load_rows(source, half, pieces):
+            raw = stage.tile([P, 2, 2, VOCAB], BF16, name="raw", align_bytes=64)
+            rows = source[2 * half * PAIR : 2 * (half + 1) * PAIR, :].rearrange("(b p e) v -> p b e v", b=2, e=2)
+            step = 2 // pieces
+            for b in range(0, 2, step):
+                nc.sync.dma_start(out=raw[:, b : b + step, :, :], in_=rows[:, b : b + step, :, :])
+            return raw
 
         def load_t(part):
             toks = slice(part * N, (part + 1) * N)
@@ -74,22 +75,17 @@ def tile_unembedding_backward_planes_e1_kernel(
                 in_=t_words.rearrange("g p n t -> p g (n t)").bitcast(I32)[:, :, toks],
             )
 
-        load_u(0)
-        load_u(1)
-        load_t(0)
-        load_u(2)
-        load_u(3)
-        load_t(1)
-        for g in range(TOK_PASSES):
-            nc.sync.dma_start(
-                out=h_raw[:, g, :, :],
-                in_=h[g * K_PASS : (g + 1) * K_PASS, :].rearrange("(p j) d -> p j d", j=PACK),
-            )
-        for g in range(TOK_PASSES):
-            nc.sync.dma_start(
-                out=g_codes[:, g, :].bitcast(I32),
-                in_=g_words[g].rearrange("p n t -> p (n t)").bitcast(I32),
-            )
+        for half in range(2):
+            new_raw = load_rows(u, half, 2)
+            u_raw.append(new_raw)
+            load_t(half)
+        nc.sync.dma_start(
+            out=h_raw[:].rearrange("p g j d -> p g (j d)"),
+            in_=h.rearrange("(g p j) d -> p g (j d)", p=P, j=PACK),
+        )
+        nc.sync.dma_start(
+            out=g_codes[:].bitcast(I32), in_=g_words.rearrange("g p n t -> p g (n t)").bitcast(I32)
+        )
 
         nc.vector.memset(t_plane[:].rearrange("p g n -> p (g n)").bitcast(I32), 0)
         nc.vector.memset(gain_bf[:], 0.0)
@@ -104,7 +100,7 @@ def tile_unembedding_backward_planes_e1_kernel(
                 )
 
         def quantise_u(b):
-            words = u_raw[b][:].rearrange("p e v -> p (e v)").bitcast(F32).rearrange("p (e w) -> p e w", e=2)
+            words = u_raw[b // 2][:, b % 2, :, :].rearrange("p e v -> p (e v)").bitcast(F32).rearrange("p (e w) -> p e w", e=2)
             grouped = []
             for g in range(VOC_PASSES):
                 bank = psum.tile([P, 4, P], F32, name="bank", tag="bank")
@@ -163,22 +159,14 @@ def tile_unembedding_backward_planes_e1_kernel(
             )
 
         acc_raw = []
-
-        def load_acc(b):
-            raw = stage.tile([P, 2, VOCAB], BF16, name="raw", align_bytes=64)
-            nc.sync.dma_start(
-                out=raw[:], in_=acc[b * PAIR : (b + 1) * PAIR, :].rearrange("(p e) v -> p e v", e=2)
-            )
-            acc_raw.append(raw)
-
         dx_tiles = {}
 
         def dx_part(m, f):
             toks = slice(m * P, (m + 1) * P)
-            if f == 0:
-                new_tile = dx_pool.tile([P, FEATURES], F32, name="dx_tile", align_bytes=64)
-                dx_tiles[m] = new_tile
-            dx_tile = dx_tiles[m]
+            if f == 0 and m % 2 == 0:
+                new_tile = dx_pool.tile([P, 2, FEATURES], F32, name="dx_tile", align_bytes=64)
+                dx_tiles[m // 2] = new_tile
+            dx_tile = dx_tiles[m // 2]
             cols = slice(f * N, (f + 1) * N)
             prod = psum.tile([P, N], F32, name="prod", tag="bank")
             for g in range(VOC_PASSES):
@@ -191,16 +179,23 @@ def tile_unembedding_backward_planes_e1_kernel(
                     start=(g == 0),
                     stop=(g == VOC_PASSES - 1),
                 )
-            nc.vector.tensor_tensor(out=dx_tile[:, cols], in0=prod[:], in1=gain_all[:, cols], op=MULT)
-            if f == 1:
-                nc.sync.dma_start(out=dx[toks, :], in_=dx_tile[:])
+            nc.vector.tensor_tensor(out=dx_tile[:, m % 2, cols], in0=prod[:], in1=gain_all[:, cols], op=MULT)
+            if f == 1 and m % 2 == 1:
+                nc.sync.dma_start(
+                    out=dx[(m - 1) * P : (m + 1) * P, :].rearrange("(i p) d -> p i d", i=2), in_=dx_tile[:]
+                )
 
         def dx_rows(m):
             dx_part(m, 0)
             dx_part(m, 1)
 
+        du_tiles = {}
+
         def du_rows(b, e):
-            du_tile = du_pool.tile([P, VOCAB], F32, name="du_tile", align_bytes=64)
+            if e == 0:
+                new_tile = du_pool.tile([P, 2, VOCAB], F32, name="du_tile", align_bytes=64)
+                du_tiles[b] = new_tile
+            du_tile = du_tiles[b]
             feats = slice((2 * b + e) * P, (2 * b + e + 1) * P)
             for n in range(VOCAB // N):
                 cols = slice(n * N, (n + 1) * N)
@@ -216,35 +211,39 @@ def tile_unembedding_backward_planes_e1_kernel(
                         stop=(g == TOK_PASSES - 1),
                     )
                 nc.vector.tensor_tensor(
-                    out=du_tile[:, cols], in0=prod[:], in1=acc_raw[b][:, e, cols], op=ADD
+                    out=du_tile[:, e, cols], in0=prod[:], in1=acc_raw[b // 2][:, b % 2, e, cols], op=ADD
                 )
             rows = du[b * PAIR : (b + 1) * PAIR, :].rearrange("(p e) v -> p e v", e=2)
-            nc.sync.dma_start(out=rows[:, e, :], in_=du_tile[:])
+            if b == PAIRS - 1:
+                nc.sync.dma_start(out=rows[:, e, :], in_=du_tile[:, e, :])
+            elif e == 1:
+                nc.sync.dma_start(out=rows, in_=du_tile[:])
 
         dx_part(0, 0)
         dx_part(1, 0)
-        quantise_u(2)
         dx_part(2, 0)
+        quantise_u(2)
         dx_part(3, 0)
         quantise_u(3)
-        load_acc(0)
-        load_acc(1)
+        for half in range(2):
+            new_raw = load_rows(acc, half, 1)
+            acc_raw.append(new_raw)
+        dx_part(4, 0)
+        dx_part(5, 0)
         dx_part(0, 1)
         dx_part(1, 1)
         dx_part(2, 1)
-        load_acc(2)
-        dx_part(3, 1)
-        dx_rows(4)
         quantise_h(0, 0)
-        load_acc(3)
-        dx_rows(5)
+        dx_part(3, 1)
+        dx_part(4, 1)
         quantise_h(1, 0)
+        dx_part(5, 1)
         dx_rows(6)
         quantise_h(0, 1)
         du_rows(0, 0)
         quantise_h(1, 1)
         dx_rows(7)
-        for b in range(PAIRS):
+        du_rows(0, 1)
+        for b in range(1, PAIRS):
             for e in range(2):
-                if (b, e) != (0, 0):
-                    du_rows(b, e)
+                du_rows(b, e)

@@ -60,12 +60,12 @@ def tile_unembedding_backward_planes_e1_kernel(
 
         u_raw = []
 
-        def load_rows(source, half, pieces):
+        def load_rows(queue, source, half, pieces):
             raw = stage.tile([P, 2, 2, VOCAB], BF16, name="raw", align_bytes=64)
             rows = source[2 * half * PAIR : 2 * (half + 1) * PAIR, :].rearrange("(b p e) v -> p b e v", b=2, e=2)
             step = 2 // pieces
             for b in range(0, 2, step):
-                nc.sync.dma_start(out=raw[:, b : b + step, :, :], in_=rows[:, b : b + step, :, :])
+                queue.dma_start(out=raw[:, b : b + step, :, :], in_=rows[:, b : b + step, :, :])
             return raw
 
         def load_t(part):
@@ -76,15 +76,12 @@ def tile_unembedding_backward_planes_e1_kernel(
             )
 
         for half in range(2):
-            new_raw = load_rows(u, half, 2)
+            new_raw = load_rows(nc.sync, u, half, 2)
             u_raw.append(new_raw)
             load_t(half)
         nc.sync.dma_start(
             out=h_raw[:].rearrange("p g j d -> p g (j d)"),
             in_=h.rearrange("(g p j) d -> p g (j d)", p=P, j=PACK),
-        )
-        nc.sync.dma_start(
-            out=g_codes[:].bitcast(I32), in_=g_words.rearrange("g p n t -> p g (n t)").bitcast(I32)
         )
 
         nc.vector.memset(t_plane[:].rearrange("p g n -> p (g n)").bitcast(I32), 0)
@@ -92,12 +89,14 @@ def tile_unembedding_backward_planes_e1_kernel(
         nc.vector.memset(g_plane[:].rearrange("p g n -> p (g n)").bitcast(I32), 0)
         nc.scalar.dma_start(out=gain_bf[0 : FEATURES // P, :], in_=gain.rearrange("(c p) -> c p", p=P))
         make_identity(nc, ident[:])
-        for queue, plane, rows in ((nc.scalar, t_plane, t_scales), (nc.gpsimd, g_plane, g_scales)):
+        def load_scales(plane, rows):
             for r in range(PACK):
-                queue.dma_start(
+                nc.scalar.dma_start(
                     out=plane[r:P:32, :, :].bitcast(I32),
                     in_=rows.bitcast(I32).rearrange("g (q r) n -> r q g n", r=PACK)[r],
                 )
+
+        load_scales(t_plane, t_scales)
 
         def quantise_u(b):
             words = u_raw[b // 2][:, b % 2, :, :].rearrange("p e v -> p (e v)").bitcast(F32).rearrange("p (e w) -> p e w", e=2)
@@ -214,10 +213,8 @@ def tile_unembedding_backward_planes_e1_kernel(
                     out=du_tile[:, e, cols], in0=prod[:], in1=acc_raw[b // 2][:, b % 2, e, cols], op=ADD
                 )
             rows = du[b * PAIR : (b + 1) * PAIR, :].rearrange("(p e) v -> p e v", e=2)
-            if b == PAIRS - 1:
-                nc.sync.dma_start(out=rows[:, e, :], in_=du_tile[:, e, :])
-            elif e == 1:
-                nc.sync.dma_start(out=rows, in_=du_tile[:])
+            queue = (nc.sync, nc.scalar)[e]
+            queue.dma_start(out=rows[:, e, :], in_=du_tile[:, e, :])
 
         dx_part(0, 0)
         dx_part(1, 0)
@@ -225,9 +222,12 @@ def tile_unembedding_backward_planes_e1_kernel(
         quantise_u(2)
         dx_part(3, 0)
         quantise_u(3)
-        for half in range(2):
-            new_raw = load_rows(acc, half, 1)
-            acc_raw.append(new_raw)
+        nc.scalar.dma_start(
+            out=g_codes[:].bitcast(I32), in_=g_words.rearrange("g p n t -> p g (n t)").bitcast(I32)
+        )
+        load_scales(g_plane, g_scales)
+        first_acc = load_rows(nc.sync, acc, 0, 1)
+        acc_raw.append(first_acc)
         dx_part(4, 0)
         dx_part(5, 0)
         dx_part(0, 1)
@@ -235,14 +235,16 @@ def tile_unembedding_backward_planes_e1_kernel(
         dx_part(2, 1)
         quantise_h(0, 0)
         dx_part(3, 1)
+        second_acc = load_rows(nc.scalar, acc, 1, 1)
+        acc_raw.append(second_acc)
         dx_part(4, 1)
         quantise_h(1, 0)
         dx_part(5, 1)
         dx_rows(6)
         quantise_h(0, 1)
         du_rows(0, 0)
-        quantise_h(1, 1)
         dx_rows(7)
+        quantise_h(1, 1)
         du_rows(0, 1)
         for b in range(1, PAIRS):
             for e in range(2):

from contextlib import ExitStack

import concourse.mybir as mybir
from concourse.masks import make_identity

TOKENS, VOCAB, FEATURES = 1024, 2048, 1024
FLOPS = 2 * 2 * TOKENS * VOCAB * FEATURES

F32 = mybir.dt.float32
BF16 = mybir.dt.bfloat16
U32 = mybir.dt.uint32
I32 = mybir.dt.int32
U8 = mybir.dt.uint8
E4M3 = mybir.dt.float8_e4m3fn_x4
E5M2 = mybir.dt.float8_e5m2_x4
ADD = mybir.AluOpType.add
MULT = mybir.AluOpType.mult

P = 128
PACK = 4
K_PASS = P * PACK
N = 512
PAIR = 2 * P
PAIRS = FEATURES // PAIR
TOK_PASSES = TOKENS // K_PASS
VOC_PASSES = VOCAB // K_PASS
TOK_TILES = TOKENS // P


def tile_unembedding_backward_planes_e1_kernel(
    tc, g_words, g_scales, t_words, t_scales, h, u, acc, gain, du, dx
):
    nc = tc.nc
    with ExitStack() as ctx:
        ctx.enter_context(tc.manual_schedule())
        keep = ctx.enter_context(tc.tile_pool(name="keep", bufs=1))
        stage = ctx.enter_context(tc.tile_pool(name="stage", bufs=2))
        work = ctx.enter_context(tc.tile_pool(name="work", bufs=4))
        dx_pool = ctx.enter_context(tc.tile_pool(name="dx_pool", bufs=4))
        du_pool = ctx.enter_context(tc.tile_pool(name="du_pool", bufs=3))
        psum = ctx.enter_context(tc.psum_pool(name="psum", bufs=8))

        t_codes = []
        for part in range(TOKENS // N):
            codes = keep.tile([P, VOC_PASSES, N], U32, name="t_codes_%d" % part, align_bytes=64)
            t_codes.append(codes)
        t_plane = keep.tile([P, VOC_PASSES, TOKENS], U8, name="t_plane", align_bytes=64)
        g_codes = keep.tile([P, TOK_PASSES, VOCAB], U32, name="g_codes", align_bytes=64)
        g_plane = keep.tile([P, TOK_PASSES, VOCAB], U8, name="g_plane", align_bytes=64)
        u_codes = keep.tile([P, VOC_PASSES, FEATURES], U32, name="u_codes", align_bytes=64)
        u_plane = keep.tile([P, VOC_PASSES, FEATURES], U8, name="u_plane", align_bytes=64)
        h_codes = keep.tile([P, TOK_PASSES, FEATURES], U32, name="h_codes", align_bytes=64)
        h_plane = keep.tile([P, TOK_PASSES, FEATURES], U8, name="h_plane", align_bytes=64)
        h_raw = keep.tile([P, TOK_PASSES, PACK, FEATURES], BF16, name="h_raw", align_bytes=64)
        ident = keep.tile([P, P], F32, name="ident")
        gain_bf = keep.tile([P, P], BF16, name="gain_bf")
        gain_rows = keep.tile([P, P], F32, name="gain_rows")
        gain_cols = keep.tile([P, FEATURES // P], F32, name="gain_cols")
        gain_all = keep.tile([P, FEATURES], F32, name="gain_all")

        u_raw = []

        def load_rows(queue, source, half, pieces):
            raw = stage.tile([P, 2, 2, VOCAB], BF16, name="raw", align_bytes=64)
            rows = source[2 * half * PAIR : 2 * (half + 1) * PAIR, :].rearrange("(b p e) v -> p b e v", b=2, e=2)
            step = 2 // pieces
            for b in range(0, 2, step):
                queue.dma_start(out=raw[:, b : b + step, :, :], in_=rows[:, b : b + step, :, :])
            return raw

        def load_t(part):
            toks = slice(part * N, (part + 1) * N)
            nc.sync.dma_start(
                out=t_codes[part][:].bitcast(I32),
                in_=t_words.rearrange("g p n t -> p g (n t)").bitcast(I32)[:, :, toks],
            )

        for half in range(2):
            new_raw = load_rows(nc.sync, u, half, 2)
            u_raw.append(new_raw)
            load_t(half)
        nc.sync.dma_start(
            out=h_raw[:].rearrange("p g j d -> p g (j d)"),
            in_=h.rearrange("(g p j) d -> p g (j d)", p=P, j=PACK),
        )

        nc.vector.memset(t_plane[:].rearrange("p g n -> p (g n)").bitcast(I32), 0)
        nc.vector.memset(gain_bf[:], 0.0)
        nc.vector.memset(g_plane[:].rearrange("p g n -> p (g n)").bitcast(I32), 0)
        nc.scalar.dma_start(out=gain_bf[0 : FEATURES // P, :], in_=gain.rearrange("(c p) -> c p", p=P))
        make_identity(nc, ident[:])
        def load_scales(plane, rows):
            for r in range(PACK):
                nc.scalar.dma_start(
                    out=plane[r:P:32, :, :].bitcast(I32),
                    in_=rows.bitcast(I32).rearrange("g (q r) n -> r q g n", r=PACK)[r],
                )

        load_scales(t_plane, t_scales)

        def quantise_u(b):
            words = u_raw[b // 2][:, b % 2, :, :].rearrange("p e v -> p (e v)").bitcast(F32).rearrange("p (e w) -> p e w", e=2)
            grouped = []
            for g in range(VOC_PASSES):
                bank = psum.tile([P, 4, P], F32, name="bank", tag="bank")
                for e in range(2):
                    for half in range(2):
                        nc.tensor.transpose(
                            bank[:, 2 * e + half, :],
                            words[:, e, g * PAIR + half : (g + 1) * PAIR : 2],
                            ident[:],
                        )
                tile = work.tile([P, PAIR * PACK], BF16, name="u_grouped", align_bytes=64)
                src = bank[:].rearrange("p q r -> p r q")
                dst = tile[:].bitcast(F32).rearrange("p (r q) -> p r q", q=4)
                if g % 2 == 0:
                    nc.scalar.copy(out=dst, in_=src)
                else:
                    nc.vector.tensor_copy(out=dst, in_=src)
                grouped.append(tile)
            for g in range(VOC_PASSES):
                cols = slice(b * PAIR, (b + 1) * PAIR)
                nc.vector.quantize_mx(
                    out=u_codes[:, g, cols].bitcast(E4M3), scales=u_plane[:, g, cols], in_=grouped[g][:]
                )

        quantise_u(0)

        nc.vector.tensor_copy(out=gain_rows[:], in_=gain_bf[:])
        bank = psum.tile([P, 4, P], F32, name="bank", tag="bank")
        nc.tensor.transpose(bank[:, 0, :], gain_rows[:], ident[:])
        nc.vector.tensor_copy(out=gain_cols[:], in_=bank[:, 0, 0 : FEATURES // P])
        for c0 in range(0, FEATURES // P, 4):
            bank = psum.tile([P, 4, P], F32, name="bank", tag="bank")
            for c in range(4):
                nc.tensor.transpose(
                    bank[:, c, :], gain_cols[:, c0 + c : c0 + c + 1].to_broadcast([P, P]), ident[:]
                )
            nc.scalar.copy(
                out=gain_all[:, c0 * P : (c0 + 4) * P], in_=bank[:].rearrange("p q r -> p (q r)")
            )

        quantise_u(1)

        def quantise_h(g, half):
            tile = work.tile([P, N, PACK], BF16, name="h_grouped", bufs=2, align_bytes=64)
            for b in range(2):
                src = h_raw[:, g, :, (2 * half + b) * PAIR : (2 * half + b + 1) * PAIR]
                nc.scalar.copy(
                    out=tile[:, b * PAIR : (b + 1) * PAIR, :].rearrange("p (e m) j -> p e m j", e=2),
                    in_=src.rearrange("p j (m e) -> p e m j", e=2),
                )
            cols = slice(half * N, (half + 1) * N)
            nc.vector.quantize_mx(
                out=h_codes[:, g, cols].bitcast(E4M3),
                scales=h_plane[:, g, cols],
                in_=tile[:].rearrange("p c j -> p (c j)"),
            )

        acc_raw = []
        dx_tiles = {}

        def dx_part(m, f):
            toks = slice(m * P, (m + 1) * P)
            if f == 0 and m % 2 == 0:
                new_tile = dx_pool.tile([P, 2, FEATURES], F32, name="dx_tile", align_bytes=64)
                dx_tiles[m // 2] = new_tile
            dx_tile = dx_tiles[m // 2]
            cols = slice(f * N, (f + 1) * N)
            prod = psum.tile([P, N], F32, name="prod", tag="bank")
            for g in range(VOC_PASSES):
                nc.tensor.matmul_mx(
                    out=prod[:],
                    lhsT=t_codes[m // 4][:, g, (m % 4) * P : (m % 4 + 1) * P].bitcast(E5M2),
                    lhsT_scale=t_plane[:, g, toks],
                    rhs=u_codes[:, g, cols].bitcast(E4M3),
                    rhs_scale=u_plane[:, g, cols],
                    start=(g == 0),
                    stop=(g == VOC_PASSES - 1),
                )
            nc.vector.tensor_tensor(out=dx_tile[:, m % 2, cols], in0=prod[:], in1=gain_all[:, cols], op=MULT)
            if f == 1 and m % 2 == 1:
                nc.sync.dma_start(
                    out=dx[(m - 1) * P : (m + 1) * P, :].rearrange("(i p) d -> p i d", i=2), in_=dx_tile[:]
                )

        def dx_rows(m):
            dx_part(m, 0)
            dx_part(m, 1)

        du_tiles = {}

        def du_rows(b, e):
            if e == 0:
                new_tile = du_pool.tile([P, 2, VOCAB], F32, name="du_tile", align_bytes=64)
                du_tiles[b] = new_tile
            du_tile = du_tiles[b]
            feats = slice((2 * b + e) * P, (2 * b + e + 1) * P)
            for n in range(VOCAB // N):
                cols = slice(n * N, (n + 1) * N)
                prod = psum.tile([P, N], F32, name="prod", tag="bank")
                for g in range(TOK_PASSES):
                    nc.tensor.matmul_mx(
                        out=prod[:],
                        lhsT=h_codes[:, g, feats].bitcast(E4M3),
                        lhsT_scale=h_plane[:, g, feats],
                        rhs=g_codes[:, g, cols].bitcast(E5M2),
                        rhs_scale=g_plane[:, g, cols],
                        start=(g == 0),
                        stop=(g == TOK_PASSES - 1),
                    )
                nc.vector.tensor_tensor(
                    out=du_tile[:, e, cols], in0=prod[:], in1=acc_raw[b // 2][:, b % 2, e, cols], op=ADD
                )
            rows = du[b * PAIR : (b + 1) * PAIR, :].rearrange("(p e) v -> p e v", e=2)
            queue = (nc.sync, nc.scalar)[e]
            queue.dma_start(out=rows[:, e, :], in_=du_tile[:, e, :])

        dx_part(0, 0)
        dx_part(1, 0)
        dx_part(2, 0)
        quantise_u(2)
        dx_part(3, 0)
        quantise_u(3)
        nc.scalar.dma_start(
            out=g_codes[:].bitcast(I32), in_=g_words.rearrange("g p n t -> p g (n t)").bitcast(I32)
        )
        load_scales(g_plane, g_scales)
        first_acc = load_rows(nc.sync, acc, 0, 1)
        acc_raw.append(first_acc)
        dx_part(4, 0)
        dx_part(5, 0)
        dx_part(0, 1)
        dx_part(1, 1)
        dx_part(2, 1)
        quantise_h(0, 0)
        dx_part(3, 1)
        second_acc = load_rows(nc.scalar, acc, 1, 1)
        acc_raw.append(second_acc)
        dx_part(4, 1)
        quantise_h(1, 0)
        dx_part(5, 1)
        dx_rows(6)
        quantise_h(0, 1)
        du_rows(0, 0)
        dx_rows(7)
        quantise_h(1, 1)
        du_rows(0, 1)
        for b in range(1, PAIRS):
            for e in range(2):
                du_rows(b, e)
